import numpy as np
import ml_dtypes


def mxq(x, axis, fmt="e4m3"):
    dtype, down = {"e4m3": (ml_dtypes.float8_e4m3fn, 7), "e5m2": (ml_dtypes.float8_e5m2, 14)}[fmt]
    v = np.moveaxis(np.asarray(x, np.float32).astype(ml_dtypes.bfloat16).astype(np.float64), axis, -1)
    blocks = v.reshape(v.shape[:-1] + (-1, 32))
    amax = np.abs(blocks).max(-1, keepdims=True)
    byte = np.maximum(np.where(amax > 0, np.frexp(amax)[1] - 1 + 127, 0) - down, 1)
    scale = np.exp2(byte - 127.0)
    codes = (blocks / scale).astype(np.float32).astype(dtype).astype(np.float64)
    return np.moveaxis((codes * scale).reshape(v.shape), -1, axis)


WIDE = False


def mx_kscale(k):
    if not WIDE:
        return np.ones(k)
    levels = np.array([10, -10, 5, -5, 0])
    if k % 512:
        return np.exp2(np.random.permutation(np.resize(levels, k // 32))).repeat(32)
    a = np.empty((k // 512, 16))
    for p in range(k // 512):
        a[p, :8] = np.random.permutation(np.resize(levels, 8))
        for g in range(8):
            far = levels[np.abs(levels - a[p, g]) >= 10]
            a[p, g + 8] = far[np.random.randint(len(far))]
    return np.exp2(a.ravel()).repeat(32)


def f64(x):
    return np.asarray(x).astype(np.float64)


def striped(idx):
    return np.tile(np.asarray(idx).reshape(-1, 16).T, (8, 1)).astype(np.uint16)


def unstriped(offs):
    return offs[:16].T.reshape(-1).astype(np.int64)


E2M1 = np.array([0.0, 0.5, 1.0, 1.5, 2.0, 3.0, 4.0, 6.0, -0.0, -0.5, -1.0, -1.5, -2.0, -3.0, -4.0, -6.0])


def pack_weight(w, fmt):
    k, n = w.shape
    w = f64(np.asarray(w, np.float32).astype(ml_dtypes.bfloat16)).reshape(k // 32, 32, n)
    amax = np.abs(w).max(1)
    if fmt == "e4m3":
        byte = np.frexp(amax)[1] - 1 + 127 - 7
    else:
        mant, ex = np.frexp(amax / 6.0)
        byte = np.where(mant > 0.5, ex, ex - 1) + 127
    byte = np.clip(np.where(amax > 0, byte, 1), 1, 254)
    scaled = (w * np.exp2(127.0 - byte)[:, None, :]).reshape(k, n).astype(np.float32)
    by_word = np.ascontiguousarray(scaled.reshape(k // 512, 128, 4, n).transpose(0, 1, 3, 2))
    if fmt == "e4m3":
        words = by_word.astype(ml_dtypes.float8_e4m3fn).view(np.uint8)
    else:
        c = by_word.astype(ml_dtypes.float4_e2m1fn).view(np.uint8) & 0xF
        words = (c[..., 0::2] | (c[..., 1::2] << 4)).reshape(k // 512, 128, 2 * n)
    return np.ascontiguousarray(words), np.ascontiguousarray(byte.astype(np.uint8).reshape(k // 512, 16, n))


def unpack_weight(words, scales, fmt):
    g, _, n = scales.shape
    words = np.ascontiguousarray(words).reshape(g, 128, n, -1)
    if fmt == "e4m3":
        vals = words.view(ml_dtypes.float8_e4m3fn).astype(np.float64)
    else:
        nib = np.empty((g, 128, n, 4), np.uint8)
        nib[..., 0::2] = words & 0xF
        nib[..., 1::2] = words >> 4
        vals = E2M1[nib]
    vals = vals * np.repeat(np.exp2(scales.astype(np.float64) - 127.0), 8, axis=1)[..., None]
    return vals.transpose(0, 1, 3, 2).reshape(g * 512, n)


def sigmoid(v):
    return 1.0 / (1.0 + np.exp(-v))


D, T, I, Q, E, G, U = 512, 2048, 1024, 128, 512, 128, 512


def setup_inputs():
    n = np.random.standard_normal
    idx = np.random.permutation(T)[:I]
    idx2 = np.random.randint(0, U, G)
    fd = mx_kscale(D)
    fi = mx_kscale(I)
    ti = np.ones(T)
    ti[idx] = fi
    keysp = pack_weight(n((D, T)) / fd[:, None], "e4m3")
    return {
        "query": (n((D, Q)) * 0.5 / np.sqrt(D) * fd[:, None]).astype(np.float32),
        "keys_words": keysp[0],
        "keys_scales": keysp[1],
        "kind": (0.4 * n((Q, U))).astype(np.float32),
        "size": (np.random.uniform(4.0, 16.0, (1, I)) * fi).astype(np.float32),
        "vals": (n((E, T)) / ti).astype(np.float32),
        "offs": striped(idx),
        "offs2": striped(idx2),
    }


def reference(query, keys_words, keys_scales, kind, size, vals, offs, offs2):
    idx = unstriped(offs)
    idx2 = unstriped(offs2)
    keysu = unpack_weight(keys_words, keys_scales, "e4m3")
    queryq = mxq(f64(query), 0, "e4m3")
    keysidxg = keysu[:, idx]
    a = queryq.T @ keysidxg
    s = a.reshape(Q, G, I // G).mean(axis=2) + f64(kind)[:, idx2]
    p = np.exp(s - np.max(s, axis=1, keepdims=True))
    r = p / np.sum(p, axis=1, keepdims=True)
    rr = np.repeat(r, I // G, axis=1)
    w = rr * sigmoid(a) * f64(size)
    wt = w.T
    vt = f64(vals)[:, idx].T
    wtq = mxq(wt, 0, "e4m3")
    vtq = mxq(vt, 0, "e4m3")
    o = wtq.T @ vtq
    return o

@@ -1,0 +1,261 @@
+from contextlib import ExitStack
+
+import concourse.mybir as mybir
+from concourse.masks import make_identity
+
+D, T, I, Q, E, G, U = 512, 2048, 1024, 128, 512, 128, 512
+FLOPS = 2 * Q * I * D + 2 * Q * I * E
+
+F32 = mybir.dt.float32
+BF16 = mybir.dt.bfloat16
+I32 = mybir.dt.int32
+U32 = mybir.dt.uint32
+U16 = mybir.dt.uint16
+U8 = mybir.dt.uint8
+FP8X4 = mybir.dt.float8_e4m3fn_x4
+ALU = mybir.AluOpType
+ACT = mybir.ActivationFunctionType
+AX = mybir.AxisListType
+
+P = 128
+PACK = 4
+PASS = P * PACK
+PASSES = I // PASS
+SPAN = I // G
+BLOCKS = E // P
+LIST_COLS = PASS // 16
+SCALAR_BLOCKS = {0: (0, 1), 1: (0,)}
+
+
+def tile_attend_spanread_kernel(tc, query, keys_words, keys_scales, kind, size, vals, offs, offs2, out):
+    nc = tc.nc
+    with ExitStack() as ctx:
+        keep = ctx.enter_context(tc.tile_pool(name="keep", bufs=1))
+        psum = ctx.enter_context(tc.psum_pool(name="psum", bufs=1))
+        turn = ctx.enter_context(tc.psum_pool(name="turn", bufs=3))
+
+        def sb(name, shape, dtype, tag=None):
+            return keep.tile(shape, dtype, name=name, tag=tag or name, align_bytes=64)
+
+        slot_list = keep.tile([P, I // 16], U16, name="slot_list")
+        kind_list = keep.tile([P, G // 16], U16, name="kind_list")
+
+        def slots(g):
+            return slot_list[:, g * LIST_COLS : (g + 1) * LIST_COLS]
+
+        key_bytes = sb("key_bytes", [P, T], U8)
+        nc.gpsimd.memset(key_bytes[:].bitcast(I32), 0)
+        warm = sb("warm", [P, 1], F32)
+        nc.vector.memset(warm[:], 0.0)
+        warm_out = sb("warm_out", [P, 1], F32)
+        nc.scalar.activation(warm_out[:], warm[:], ACT.Sigmoid)
+        identity = sb("identity", [P, P], F32)
+        make_identity(nc, identity[:])
+
+        nc.sync.dma_start(slot_list[:], offs)
+        for quad in range(4):
+            nc.sync.dma_start(
+                key_bytes[32 * quad : 32 * quad + 4, :].bitcast(I32),
+                keys_scales[0, 4 * quad : 4 * quad + 4, :].bitcast(I32),
+            )
+        query_raw = sb("query_raw", [P, PACK, Q], F32)
+        nc.sync.dma_start(query_raw[:], query.rearrange("(p j) q -> p j q", j=PACK))
+        key_words = sb("key_words", [P, T], I32)
+        nc.sync.dma_start(key_words[:], keys_words[0].rearrange("p n t -> p (n t)").bitcast(I32))
+
+        windows = {}
+        staged = {}
+
+        def load_half(b, h):
+            staged[b, h] = sb("stage%d_%d" % (b, h), [P, T // 2], F32)
+            nc.sync.dma_start(staged[b, h][:], vals[b * P : (b + 1) * P, h * (T // 2) : (h + 1) * (T // 2)])
+
+        def load_block(b):
+            windows[b] = sb("window%d" % b, [P, T], F32)
+            nc.sync.dma_start(windows[b][:], vals[b * P : (b + 1) * P, :])
+
+        load_half(0, 0)
+        kind_pool = sb("kind_pool", [P, U], F32)
+        nc.sync.dma_start(kind_pool[:], kind)
+        nc.sync.dma_start(kind_list[:], offs2)
+        size_col = sb("size_col", [P, PASSES, PACK], F32)
+        nc.sync.dma_start(size_col[:], size.rearrange("o (g p t) -> p (o g) t", g=PASSES, t=PACK))
+        load_half(0, 1)
+        load_block(2)
+        load_half(1, 0)
+        load_half(1, 1)
+        load_block(3)
+
+        def cast_block(b):
+            windows[b] = sb("window%d" % b, [P, T], BF16)
+            for h in range(2):
+                nc.scalar.activation(windows[b][:, h * (T // 2) : (h + 1) * (T // 2)], staged[b, h][:], ACT.Copy)
+
+        picked = {}
+
+        def gather_values(b, g, tag=None):
+            picked[b, g] = sb("picked%d_%d" % (b, g), [P, PASS], BF16, tag)
+            if g in SCALAR_BLOCKS.get(b, ()):
+                nc.scalar.activation(picked[b, g][:], windows[b][:].indirect(slots(g)), ACT.Copy)
+            else:
+                nc.vector.tensor_copy(picked[b, g][:], windows[b][:].indirect(slots(g)))
+
+        def turn_values(b, passes, into):
+            n = len(passes)
+            bank = turn.tile([P, PASSES, 2, P], F32, name="v_bank", tag="v_bank")
+            for j, g in enumerate(passes):
+                words = picked[b, g][:].bitcast(F32)
+                for u in range(2):
+                    nc.tensor.transpose(bank[:, j, u, :], words[:, u : 2 * P : 2], identity[:])
+            nc.scalar.copy(into, bank[:, 0:n].rearrange("p g u e -> p g e u"))
+
+        def quantise_values(name, grouped):
+            width = grouped.shape[1] * grouped.shape[2]
+            codes = sb("v_codes" + name, [P, width], U32)
+            scales = sb("v_scales" + name, [P, width], U8)
+            nc.vector.quantize_mx(
+                out=codes[:].bitcast(FP8X4),
+                scales=scales[:],
+                in_=grouped[:].rearrange("p g e u -> p (g e u)").bitcast(BF16),
+            )
+            return codes, scales
+
+        query_grouped = sb("query_grouped", [P, Q, PACK], BF16)
+        nc.scalar.activation(query_grouped[:], query_raw[:].rearrange("p j q -> p q j"), ACT.Copy)
+
+        picked_bytes = sb("picked_bytes", [P, I], U8)
+        nc.vector.tensor_copy(picked_bytes[:], key_bytes[:].indirect(slot_list[:]))
+        picked_words = [sb("picked_words%d" % g, [P, PASS], U32) for g in range(PASSES)]
+        q_codes = sb("q_codes", [P, Q], U32)
+        q_scales = sb("q_scales", [P, Q], U8)
+        nc.vector.tensor_copy(picked_words[0][:], key_words[:].bitcast(U32).indirect(slots(0)))
+        nc.vector.quantize_mx(
+            out=q_codes[:].bitcast(FP8X4), scales=q_scales[:], in_=query_grouped[:].rearrange("p q j -> p (q j)")
+        )
+        nc.vector.tensor_copy(picked_words[1][:], key_words[:].bitcast(U32).indirect(slots(1)))
+        scores = [psum.tile([P, PASS], F32, name="scores%d" % g, tag="ab%d" % g) for g in range(PASSES)]
+        for g in range(PASSES):
+            nc.tensor.matmul_mx(
+                out=scores[g][:],
+                lhsT=q_codes[:].bitcast(FP8X4),
+                lhsT_scale=q_scales[:],
+                rhs=picked_words[g][:].bitcast(FP8X4),
+                rhs_scale=picked_bytes[:, g * PASS : (g + 1) * PASS],
+                start=True,
+                stop=True,
+            )
+
+        cast_block(0)
+
+        span_sum = sb("span_sum", [P, G], F32)
+        gates = [sb("gates%d" % g, [P, PACK, P], F32) for g in range(PASSES)]
+
+        def sum_spans(g):
+            nc.vector.tensor_reduce(
+                span_sum[:, g * (G // PASSES) : (g + 1) * (G // PASSES)],
+                scores[g][:].rearrange("p (s j) -> p s j", j=SPAN),
+                AX.X,
+                ALU.add,
+            )
+
+        def gate(g):
+            nc.scalar.activation(gates[g][:], scores[g][:].rearrange("p (s t) -> p t s", t=PACK), ACT.Sigmoid)
+
+        sum_spans(0)
+        gate(0)
+        sum_spans(1)
+        gate(1)
+
+        picked_kind = sb("picked_kind", [P, G], F32)
+        nc.vector.tensor_copy(picked_kind[:], kind_pool[:].indirect(kind_list[:]))
+        logits = sb("logits", [P, G], F32)
+        nc.vector.scalar_tensor_tensor(logits[:], span_sum[:], 1.0 / SPAN, picked_kind[:], ALU.mult, ALU.add)
+        minus_max = sb("minus_max", [P, 1], F32)
+        nc.vector.tensor_reduce(minus_max[:], logits[:], AX.X, ALU.max, negate=True)
+        span_exp = sb("span_exp", [P, G], F32)
+        row_sum = sb("row_sum", [P, 1], F32)
+        nc.scalar.activation(span_exp[:], logits[:], ACT.Exp, bias=minus_max[:], accum_out=row_sum[:])
+
+        gates_turned = [psum.tile([P, PACK, Q], F32, name="gates_turned%d" % g) for g in range(PASSES)]
+        for g in range(PASSES):
+            for t in range(PACK):
+                nc.tensor.transpose(gates_turned[g][:, t, :], gates[g][:, t, :], identity[:])
+
+        gather_values(0, 0, "logits")
+        gather_values(0, 1)
+        gather_values(2, 0)
+
+        sized = sb("sized", [P, PASSES, Q, PACK], F32)
+        for g in range(PASSES):
+            nc.vector.tensor_tensor(
+                sized[:, g],
+                gates_turned[g][:].rearrange("p t q -> p q t"),
+                size_col[:, g, :].unsqueeze(1).to_broadcast([P, Q, PACK]),
+                ALU.mult,
+            )
+
+        inv_sum = sb("inv_sum", [P, 1], F32)
+        nc.vector.reciprocal(inv_sum[:], row_sum[:])
+        span_weight = sb("span_weight", [P, G, 2], F32)
+        nc.vector.tensor_scalar(
+            span_weight[:], span_exp[:].unsqueeze(2).to_broadcast([P, G, 2]), inv_sum[:], None, ALU.mult
+        )
+        weight_turned = psum.tile([P, PASSES, Q], F32, name="weight_turned")
+        twice = span_weight[:].rearrange("p s k -> p (s k)")
+        for g in range(PASSES):
+            nc.tensor.transpose(weight_turned[:, g, :], twice[:, g * P : (g + 1) * P], identity[:])
+
+        gather_values(2, 1)
+        grouped_lo = [sb("grouped_lo%d" % g, [P, 1, 2 * P, 2], F32) for g in range(PASSES)]
+        grouped_hi = sb("grouped_hi", [P, PASSES, 2 * P, 2], F32)
+        turn_values(0, (0,), grouped_lo[0][:, :, 0:P, :])
+        turn_values(0, (1,), grouped_lo[1][:, :, 0:P, :])
+
+        w_grouped = sb("w_grouped", [P, PASSES * Q, PACK], BF16)
+        nc.vector.tensor_tensor(
+            w_grouped[:],
+            sized[:].rearrange("p g q t -> p (g q) t"),
+            weight_turned[:].rearrange("p g q -> p (g q)").unsqueeze(2).to_broadcast([P, PASSES * Q, PACK]),
+            ALU.mult,
+        )
+        turn_values(2, (0, 1), grouped_hi[:, :, 0:P, :])
+        w_codes = sb("w_codes", [P, PASSES * Q], U32)
+        w_scales = sb("w_scales", [P, PASSES * Q], U8)
+        nc.vector.quantize_mx(
+            out=w_codes[:].bitcast(FP8X4), scales=w_scales[:], in_=w_grouped[:].rearrange("p n t -> p (n t)")
+        )
+
+        cast_block(1)
+        gather_values(3, 0)
+        gather_values(3, 1)
+        gather_values(1, 0)
+        turn_values(3, (0, 1), grouped_hi[:, :, P : 2 * P, :])
+        gather_values(1, 1, "window3")
+        turn_values(1, (1,), grouped_lo[1][:, :, P : 2 * P, :])
+        turn_values(1, (0,), grouped_lo[0][:, :, P : 2 * P, :])
+        c_hi, s_hi = quantise_values("hi", grouped_hi)
+        c1, s1 = quantise_values("lo1", grouped_lo[1])
+        c0, s0 = quantise_values("lo0", grouped_lo[0])
+
+        def multiply(sums, operands):
+            for j, (g, codes, scales) in enumerate(operands):
+                nc.tensor.matmul_mx(
+                    out=sums,
+                    lhsT=w_codes[:, g * Q : (g + 1) * Q].bitcast(FP8X4),
+                    lhsT_scale=w_scales[:, g * Q : (g + 1) * Q],
+                    rhs=codes.bitcast(FP8X4),
+                    rhs_scale=scales,
+                    start=(j == 0),
+                    stop=(j == PASSES - 1),
+                )
+
+        sums_a = psum.tile([P, 2 * P], F32, name="sums_a", tag="ab0")
+        multiply(sums_a[:], [(g, c_hi[:, g * 2 * P : (g + 1) * 2 * P], s_hi[:, g * 2 * P : (g + 1) * 2 * P]) for g in range(PASSES)])
+        result_a = sb("result_a", [P, 2 * P], F32)
+        nc.scalar.copy(result_a[:], sums_a[:])
+        nc.sync.dma_start(out[:, 2 * P : 4 * P], result_a[:])
+        sums_b = psum.tile([P, 2 * P], F32, name="sums_b", tag="ab1")
+        multiply(sums_b[:], [(1, c1[:], s1[:]), (0, c0[:], s0[:])])
+        result_b = sb("result_b", [P, 2 * P], F32)
+        nc.vector.tensor_copy(result_b[:], sums_b[:])
+        nc.sync.dma_start(out[:, 0 : 2 * P], result_b[:])

@@ -24,7 +24,8 @@ PASSES = I // PASS
 SPAN = I // G
 BLOCKS = E // P
 LIST_COLS = PASS // 16
-SCALAR_BLOCKS = {0: (0, 1), 1: (0,)}
+HALF = E // 2
+SCALAR_BLOCK, FIRST, SECOND, LAST = 2, 0, 1, 3
 
 
 def tile_attend_spanread_kernel(tc, query, keys_words, keys_scales, kind, size, vals, offs, offs2, out):
@@ -32,7 +33,6 @@ def tile_attend_spanread_kernel(tc, query, keys_words, keys_scales, kind, size, 
     with ExitStack() as ctx:
         keep = ctx.enter_context(tc.tile_pool(name="keep", bufs=1))
         psum = ctx.enter_context(tc.psum_pool(name="psum", bufs=1))
-        turn = ctx.enter_context(tc.psum_pool(name="turn", bufs=3))
 
         def sb(name, shape, dtype, tag=None):
             return keep.tile(shape, dtype, name=name, tag=tag or name, align_bytes=64)
@@ -46,77 +46,77 @@ def tile_attend_spanread_kernel(tc, query, keys_words, keys_scales, kind, size, 
         key_bytes = sb("key_bytes", [P, T], U8)
         nc.gpsimd.memset(key_bytes[:].bitcast(I32), 0)
         warm = sb("warm", [P, 1], F32)
-        nc.vector.memset(warm[:], 0.0)
+        nc.gpsimd.memset(warm[:], 0.0)
         warm_out = sb("warm_out", [P, 1], F32)
-        nc.scalar.activation(warm_out[:], warm[:], ACT.Sigmoid)
+        nc.scalar.activation(warm_out[:], warm[:], ACT.Exp)
         identity = sb("identity", [P, P], F32)
         make_identity(nc, identity[:])
 
         nc.sync.dma_start(slot_list[:], offs)
+        nc.sync.dma_start(kind_list[:], offs2)
         for quad in range(4):
             nc.sync.dma_start(
                 key_bytes[32 * quad : 32 * quad + 4, :].bitcast(I32),
                 keys_scales[0, 4 * quad : 4 * quad + 4, :].bitcast(I32),
             )
-        query_raw = sb("query_raw", [P, PACK, Q], F32)
-        nc.sync.dma_start(query_raw[:], query.rearrange("(p j) q -> p j q", j=PACK))
         key_words = sb("key_words", [P, T], I32)
         nc.sync.dma_start(key_words[:], keys_words[0].rearrange("p n t -> p (n t)").bitcast(I32))
+        query_raw = sb("query_raw", [P, PACK, Q], F32)
+        nc.sync.dma_start(query_raw[:], query.rearrange("(p j) q -> p j q", j=PACK))
 
         windows = {}
         staged = {}
 
-        def load_half(b, h):
-            staged[b, h] = sb("stage%d_%d" % (b, h), [P, T // 2], F32)
-            nc.sync.dma_start(staged[b, h][:], vals[b * P : (b + 1) * P, h * (T // 2) : (h + 1) * (T // 2)])
+        def load_half(h):
+            staged[h] = sb("stage%d" % h, [P, T // 2], F32)
+            rows = slice(SCALAR_BLOCK * P, (SCALAR_BLOCK + 1) * P)
+            nc.sync.dma_start(staged[h][:], vals[rows, h * (T // 2) : (h + 1) * (T // 2)])
+
+        load_half(0)
+        kind_pool = sb("kind_pool", [P, U], F32)
+        nc.sync.dma_start(kind_pool[:], kind)
+        size_col = sb("size_col", [P, PASSES, PACK], F32)
+        nc.sync.dma_start(size_col[:], size.rearrange("o (g p t) -> p (o g) t", g=PASSES, t=PACK))
 
         def load_block(b):
             windows[b] = sb("window%d" % b, [P, T], F32)
             nc.sync.dma_start(windows[b][:], vals[b * P : (b + 1) * P, :])
 
-        load_half(0, 0)
-        kind_pool = sb("kind_pool", [P, U], F32)
-        nc.sync.dma_start(kind_pool[:], kind)
-        nc.sync.dma_start(kind_list[:], offs2)
-        size_col = sb("size_col", [P, PASSES, PACK], F32)
-        nc.sync.dma_start(size_col[:], size.rearrange("o (g p t) -> p (o g) t", g=PASSES, t=PACK))
-        load_half(0, 1)
-        load_block(2)
-        load_half(1, 0)
-        load_half(1, 1)
-        load_block(3)
+        load_half(1)
+        load_block(FIRST)
+        load_block(SECOND)
+        load_block(LAST)
+        windows[SCALAR_BLOCK] = sb("window_cast", [P, T], BF16)
 
-        def cast_block(b):
-            windows[b] = sb("window%d" % b, [P, T], BF16)
-            for h in range(2):
-                nc.scalar.activation(windows[b][:, h * (T // 2) : (h + 1) * (T // 2)], staged[b, h][:], ACT.Copy)
+        def cast_half(h):
+            nc.scalar.activation(windows[SCALAR_BLOCK][:, h * (T // 2) : (h + 1) * (T // 2)], staged[h][:], ACT.Copy)
 
         picked = {}
 
-        def gather_values(b, g, tag=None):
-            picked[b, g] = sb("picked%d_%d" % (b, g), [P, PASS], BF16, tag)
-            if g in SCALAR_BLOCKS.get(b, ()):
-                nc.scalar.activation(picked[b, g][:], windows[b][:].indirect(slots(g)), ACT.Copy)
+        def gather_values(b):
+            if b == SCALAR_BLOCK:
+                picked[b] = sb("picked%d" % b, [P, I], BF16)
+                nc.scalar.activation(picked[b][:], windows[b][:].indirect(slot_list[:]), ACT.Copy)
             else:
-                nc.vector.tensor_copy(picked[b, g][:], windows[b][:].indirect(slots(g)))
+                picked[b] = sb("picked%d" % b, [P, I], BF16)
+                nc.vector.tensor_copy(picked[b][:], windows[b][:].indirect(slot_list[:]))
 
-        def turn_values(b, passes, into):
-            n = len(passes)
-            bank = turn.tile([P, PASSES, 2, P], F32, name="v_bank", tag="v_bank")
-            for j, g in enumerate(passes):
-                words = picked[b, g][:].bitcast(F32)
+
+        def turn_values(b, bank_tag):
+            bank = psum.tile([P, PASSES, 2, P], F32, name="v_bank%d" % b, tag=bank_tag)
+            words = picked[b][:].bitcast(F32)
+            for g in range(PASSES):
                 for u in range(2):
-                    nc.tensor.transpose(bank[:, j, u, :], words[:, u : 2 * P : 2], identity[:])
-            nc.scalar.copy(into, bank[:, 0:n].rearrange("p g u e -> p g e u"))
+                    nc.tensor.transpose(bank[:, g, u, :], words[:, 2 * P * g + u : 2 * P * (g + 1) : 2], identity[:])
+            nc.scalar.copy(grouped[:, :, b * P : (b + 1) * P, :], bank[:].rearrange("p g u e -> p g e u"))
 
-        def quantise_values(name, grouped):
-            width = grouped.shape[1] * grouped.shape[2]
-            codes = sb("v_codes" + name, [P, width], U32)
-            scales = sb("v_scales" + name, [P, width], U8)
+        def quantise_values(g, first, width):
+            codes = sb("v_codes%d_%d" % (g, first), [P, width], U32)
+            scales = sb("v_scales%d_%d" % (g, first), [P, width], U8)
             nc.vector.quantize_mx(
                 out=codes[:].bitcast(FP8X4),
                 scales=scales[:],
-                in_=grouped[:].rearrange("p g e u -> p (g e u)").bitcast(BF16),
+                in_=late[:, 2 * (g * E + first) : 2 * (g * E + first + width)].bitcast(BF16),
             )
             return codes, scales
 
@@ -125,15 +125,16 @@ def tile_attend_spanread_kernel(tc, query, keys_words, keys_scales, kind, size, 
 
         picked_bytes = sb("picked_bytes", [P, I], U8)
         nc.vector.tensor_copy(picked_bytes[:], key_bytes[:].indirect(slot_list[:]))
-        picked_words = [sb("picked_words%d" % g, [P, PASS], U32) for g in range(PASSES)]
+        picked_words = [sb("picked_words0", [P, PASS], U32)]
         q_codes = sb("q_codes", [P, Q], U32)
         q_scales = sb("q_scales", [P, Q], U8)
         nc.vector.tensor_copy(picked_words[0][:], key_words[:].bitcast(U32).indirect(slots(0)))
         nc.vector.quantize_mx(
             out=q_codes[:].bitcast(FP8X4), scales=q_scales[:], in_=query_grouped[:].rearrange("p q j -> p (q j)")
         )
+        picked_words.append(sb("picked_words1", [P, PASS], U32, "query_grouped"))
         nc.vector.tensor_copy(picked_words[1][:], key_words[:].bitcast(U32).indirect(slots(1)))
-        scores = [psum.tile([P, PASS], F32, name="scores%d" % g, tag="ab%d" % g) for g in range(PASSES)]
+        scores = [psum.tile([P, PASS], F32, name="scores%d" % g, tag="bank%d" % g) for g in range(PASSES)]
         for g in range(PASSES):
             nc.tensor.matmul_mx(
                 out=scores[g][:],
@@ -145,117 +146,101 @@ def tile_attend_spanread_kernel(tc, query, keys_words, keys_scales, kind, size, 
                 stop=True,
             )
 
-        cast_block(0)
+        cast_half(0)
+        picked_kind = sb("picked_kind", [P, G], F32)
+        nc.vector.tensor_copy(picked_kind[:], kind_pool[:].indirect(kind_list[:]))
 
         span_sum = sb("span_sum", [P, G], F32)
-        gates = [sb("gates%d" % g, [P, PACK, P], F32) for g in range(PASSES)]
-
-        def sum_spans(g):
+        for g in range(PASSES):
             nc.vector.tensor_reduce(
                 span_sum[:, g * (G // PASSES) : (g + 1) * (G // PASSES)],
                 scores[g][:].rearrange("p (s j) -> p s j", j=SPAN),
                 AX.X,
                 ALU.add,
             )
-
-        def gate(g):
-            nc.scalar.activation(gates[g][:], scores[g][:].rearrange("p (s t) -> p t s", t=PACK), ACT.Sigmoid)
-
-        sum_spans(0)
-        gate(0)
-        sum_spans(1)
-        gate(1)
-
-        picked_kind = sb("picked_kind", [P, G], F32)
-        nc.vector.tensor_copy(picked_kind[:], kind_pool[:].indirect(kind_list[:]))
         logits = sb("logits", [P, G], F32)
         nc.vector.scalar_tensor_tensor(logits[:], span_sum[:], 1.0 / SPAN, picked_kind[:], ALU.mult, ALU.add)
         minus_max = sb("minus_max", [P, 1], F32)
         nc.vector.tensor_reduce(minus_max[:], logits[:], AX.X, ALU.max, negate=True)
-        span_exp = sb("span_exp", [P, G], F32)
+
+        cast_half(1)
+        gather_values(SCALAR_BLOCK)
+        widths = (PASSES * 2 * E, I, I, 2 * G, G)
+        late = sb("late", [P, sum(widths)], F32, "window_cast")
+        parts = [late[:, sum(widths[:k]) : sum(widths[: k + 1])] for k in range(len(widths))]
+        grouped = parts[0].rearrange("p (g e u) -> p g e u", g=PASSES, u=2)
+        gates = parts[1].rearrange("p (g t s) -> p g t s", g=PASSES, t=PACK)
+        sized = parts[2].rearrange("p (g t q) -> p g t q", g=PASSES, t=PACK)
+        twice = parts[3]
+        span_exp = parts[4]
+
         row_sum = sb("row_sum", [P, 1], F32)
-        nc.scalar.activation(span_exp[:], logits[:], ACT.Exp, bias=minus_max[:], accum_out=row_sum[:])
-
-        gates_turned = [psum.tile([P, PACK, Q], F32, name="gates_turned%d" % g) for g in range(PASSES)]
+        nc.scalar.activation(span_exp, logits[:], ACT.Exp, bias=minus_max[:], accum_out=row_sum[:])
+        gates_turned = [psum.tile([P, PACK, Q], F32, name="gates_turned%d" % g, tag="bank%d" % (2 + g)) for g in range(PASSES)]
         for g in range(PASSES):
+            nc.scalar.activation(gates[:, g], scores[g][:].rearrange("p (s t) -> p t s", t=PACK), ACT.Sigmoid)
             for t in range(PACK):
-                nc.tensor.transpose(gates_turned[g][:, t, :], gates[g][:, t, :], identity[:])
+                nc.tensor.transpose(gates_turned[g][:, t, :], gates[:, g, t, :], identity[:])
 
-        gather_values(0, 0, "logits")
-        gather_values(0, 1)
-        gather_values(2, 0)
-
-        sized = sb("sized", [P, PASSES, Q, PACK], F32)
-        for g in range(PASSES):
-            nc.vector.tensor_tensor(
-                sized[:, g],
-                gates_turned[g][:].rearrange("p t q -> p q t"),
-                size_col[:, g, :].unsqueeze(1).to_broadcast([P, Q, PACK]),
-                ALU.mult,
-            )
-
-        inv_sum = sb("inv_sum", [P, 1], F32)
+        gather_values(FIRST)
+        inv_sum = sb("inv_sum", [P, 1], F32, "window%d" % FIRST)
         nc.vector.reciprocal(inv_sum[:], row_sum[:])
-        span_weight = sb("span_weight", [P, G, 2], F32)
-        nc.vector.tensor_scalar(
-            span_weight[:], span_exp[:].unsqueeze(2).to_broadcast([P, G, 2]), inv_sum[:], None, ALU.mult
+        nc.scalar.activation(
+            twice.rearrange("p (s k) -> p s k", k=2),
+            span_exp.unsqueeze(2).to_broadcast([P, G, 2]),
+            ACT.Copy,
+            scale=inv_sum[:],
         )
-        weight_turned = psum.tile([P, PASSES, Q], F32, name="weight_turned")
-        twice = span_weight[:].rearrange("p s k -> p (s k)")
+        weight_turned = psum.tile([P, PASSES, Q], F32, name="weight_turned", tag="bank4")
         for g in range(PASSES):
             nc.tensor.transpose(weight_turned[:, g, :], twice[:, g * P : (g + 1) * P], identity[:])
+        turn_values(FIRST, "bank5")
+        for g in range(PASSES):
+            for t in range(PACK):
+                nc.scalar.activation(
+                    sized[:, g, t, :], gates_turned[g][:, t, :], ACT.Copy, scale=size_col[:, g, t : t + 1]
+                )
+        turn_values(SCALAR_BLOCK, "bank7")
+        gather_values(SECOND)
+        turn_values(SECOND, "bank6")
+        gather_values(LAST)
+        turn_values(LAST, "bank0")
 
-        gather_values(2, 1)
-        grouped_lo = [sb("grouped_lo%d" % g, [P, 1, 2 * P, 2], F32) for g in range(PASSES)]
-        grouped_hi = sb("grouped_hi", [P, PASSES, 2 * P, 2], F32)
-        turn_values(0, (0,), grouped_lo[0][:, :, 0:P, :])
-        turn_values(0, (1,), grouped_lo[1][:, :, 0:P, :])
-
-        w_grouped = sb("w_grouped", [P, PASSES * Q, PACK], BF16)
+        w_grouped = sb("w_grouped", [P, PASSES, Q, PACK], BF16, "window%d" % LAST)
         nc.vector.tensor_tensor(
             w_grouped[:],
-            sized[:].rearrange("p g q t -> p (g q) t"),
-            weight_turned[:].rearrange("p g q -> p (g q)").unsqueeze(2).to_broadcast([P, PASSES * Q, PACK]),
+            sized.rearrange("p g t q -> p g q t"),
+            weight_turned[:].unsqueeze(3).to_broadcast([P, PASSES, Q, PACK]),
             ALU.mult,
         )
-        turn_values(2, (0, 1), grouped_hi[:, :, 0:P, :])
+        first_codes, first_scales = quantise_values(0, 0, E)
         w_codes = sb("w_codes", [P, PASSES * Q], U32)
         w_scales = sb("w_scales", [P, PASSES * Q], U8)
         nc.vector.quantize_mx(
-            out=w_codes[:].bitcast(FP8X4), scales=w_scales[:], in_=w_grouped[:].rearrange("p n t -> p (n t)")
+            out=w_codes[:].bitcast(FP8X4), scales=w_scales[:], in_=w_grouped[:].rearrange("p g q t -> p (g q t)")
         )
+        sums = [psum.tile([P, HALF], F32, name="sums%d" % h, tag="bank%d" % (2 + h)) for h in range(2)]
 
-        cast_block(1)
-        gather_values(3, 0)
-        gather_values(3, 1)
-        gather_values(1, 0)
-        turn_values(3, (0, 1), grouped_hi[:, :, P : 2 * P, :])
-        gather_values(1, 1, "window3")
-        turn_values(1, (1,), grouped_lo[1][:, :, P : 2 * P, :])
-        turn_values(1, (0,), grouped_lo[0][:, :, P : 2 * P, :])
-        c_hi, s_hi = quantise_values("hi", grouped_hi)
-        c1, s1 = quantise_values("lo1", grouped_lo[1])
-        c0, s0 = quantise_values("lo0", grouped_lo[0])
+        def multiply(g, h, codes, scales):
+            nc.tensor.matmul_mx(
+                out=sums[h][:],
+                lhsT=w_codes[:, g * Q : (g + 1) * Q].bitcast(FP8X4),
+                lhsT_scale=w_scales[:, g * Q : (g + 1) * Q],
+                rhs=codes.bitcast(FP8X4),
+                rhs_scale=scales,
+                start=(g == 0),
+                stop=(g == PASSES - 1),
+            )
 
-        def multiply(sums, operands):
-            for j, (g, codes, scales) in enumerate(operands):
-                nc.tensor.matmul_mx(
-                    out=sums,
-                    lhsT=w_codes[:, g * Q : (g + 1) * Q].bitcast(FP8X4),
-                    lhsT_scale=w_scales[:, g * Q : (g + 1) * Q],
-                    rhs=codes.bitcast(FP8X4),
-                    rhs_scale=scales,
-                    start=(j == 0),
-                    stop=(j == PASSES - 1),
-                )
-
-        sums_a = psum.tile([P, 2 * P], F32, name="sums_a", tag="ab0")
-        multiply(sums_a[:], [(g, c_hi[:, g * 2 * P : (g + 1) * 2 * P], s_hi[:, g * 2 * P : (g + 1) * 2 * P]) for g in range(PASSES)])
-        result_a = sb("result_a", [P, 2 * P], F32)
-        nc.scalar.copy(result_a[:], sums_a[:])
-        nc.sync.dma_start(out[:, 2 * P : 4 * P], result_a[:])
-        sums_b = psum.tile([P, 2 * P], F32, name="sums_b", tag="ab1")
-        multiply(sums_b[:], [(1, c1[:], s1[:]), (0, c0[:], s0[:])])
-        result_b = sb("result_b", [P, 2 * P], F32)
-        nc.vector.tensor_copy(result_b[:], sums_b[:])
-        nc.sync.dma_start(out[:, 0 : 2 * P], result_b[:])
+        for h in range(2):
+            multiply(0, h, first_codes[:, h * HALF : (h + 1) * HALF], first_scales[:, h * HALF : (h + 1) * HALF])
+        for h in range(2):
+            codes, scales = quantise_values(1, h * HALF, HALF)
+            multiply(1, h, codes[:], scales[:])
+        for h in range(2):
+            result = sb("result%d" % h, [P, HALF], F32)
+            if h == 0:
+                nc.scalar.copy(result[:], sums[h][:])
+            else:
+                nc.vector.tensor_copy(result[:], sums[h][:])
+            nc.sync.dma_start(out[:, h * HALF : (h + 1) * HALF], result[:])

@@ -203,8 +203,14 @@ def tile_attend_spanread_kernel(tc, query, keys_words, keys_scales, kind, size, 
         turn_values(SCALAR_BLOCK, "bank7")
         gather_values(SECOND)
         turn_values(SECOND, "bank6")
-        gather_values(LAST)
-        turn_values(LAST, "bank0")
+        for g in range(PASSES):
+            part = sb("picked_last%d" % g, [P, PASS], BF16)
+            nc.vector.tensor_copy(part[:], windows[LAST][:].indirect(slots(g)))
+            bank = psum.tile([P, 2, P], F32, name="last_bank%d" % g, tag="bank%d" % g)
+            words = part[:].bitcast(F32)
+            for u in range(2):
+                nc.tensor.transpose(bank[:, u, :], words[:, u : 2 * P : 2], identity[:])
+            nc.scalar.copy(grouped[:, g, LAST * P : (LAST + 1) * P, :], bank[:].rearrange("p u e -> p e u"))
 
         w_grouped = sb("w_grouped", [P, PASSES, Q, PACK], BF16, "window%d" % LAST)
         nc.vector.tensor_tensor(
@@ -219,11 +225,12 @@ def tile_attend_spanread_kernel(tc, query, keys_words, keys_scales, kind, size, 
         nc.vector.quantize_mx(
             out=w_codes[:].bitcast(FP8X4), scales=w_scales[:], in_=w_grouped[:].rearrange("p g q t -> p (g q t)")
         )
-        sums = [psum.tile([P, HALF], F32, name="sums%d" % h, tag="bank%d" % (2 + h)) for h in range(2)]
+        groups = ((0, HALF), (HALF, P), (HALF + P, P))
+        sums = [psum.tile([P, width], F32, name="sums%d" % k, tag="bank%d" % (2 + k)) for k, (first, width) in enumerate(groups)]
 
-        def multiply(g, h, codes, scales):
+        def multiply(g, k, codes, scales):
             nc.tensor.matmul_mx(
-                out=sums[h][:],
+                out=sums[k][:],
                 lhsT=w_codes[:, g * Q : (g + 1) * Q].bitcast(FP8X4),
                 lhsT_scale=w_scales[:, g * Q : (g + 1) * Q],
                 rhs=codes.bitcast(FP8X4),
@@ -232,15 +239,14 @@ def tile_attend_spanread_kernel(tc, query, keys_words, keys_scales, kind, size, 
                 stop=(g == PASSES - 1),
             )
 
-        for h in range(2):
-            multiply(0, h, first_codes[:, h * HALF : (h + 1) * HALF], first_scales[:, h * HALF : (h + 1) * HALF])
-        for h in range(2):
-            codes, scales = quantise_values(1, h * HALF, HALF)
-            multiply(1, h, codes[:], scales[:])
-        for h in range(2):
-            result = sb("result%d" % h, [P, HALF], F32)
-            if h == 0:
-                nc.scalar.copy(result[:], sums[h][:])
-            else:
-                nc.vector.tensor_copy(result[:], sums[h][:])
-            nc.sync.dma_start(out[:, h * HALF : (h + 1) * HALF], result[:])
+        for k, (first, width) in enumerate(groups):
+            multiply(0, k, first_codes[:, first : first + width], first_scales[:, first : first + width])
+        for k, (first, width) in enumerate(groups):
+            codes, scales = quantise_values(1, first, width)
+            multiply(1, k, codes[:], scales[:])
+        result = [sb("result%d" % h, [P, HALF], F32) for h in range(2)]
+        nc.scalar.copy(result[0][:], sums[0][:])
+        nc.sync.dma_start(out[:, 0:HALF], result[0][:])
+        nc.scalar.copy(result[1][:, 0:P], sums[1][:])
+        nc.vector.tensor_copy(result[1][:, P:HALF], sums[2][:])
+        nc.sync.dma_start(out[:, HALF:E], result[1][:])

@@ -44,7 +44,7 @@ def tile_attend_spanread_kernel(tc, query, keys_words, keys_scales, kind, size, 
             return slot_list[:, g * LIST_COLS : (g + 1) * LIST_COLS]
 
         key_bytes = sb("key_bytes", [P, T], U8)
-        nc.gpsimd.memset(key_bytes[:].bitcast(I32), 0)
+        nc.vector.memset(key_bytes[:].bitcast(I32), 0)
         warm = sb("warm", [P, 1], F32)
         nc.gpsimd.memset(warm[:], 0.0)
         warm_out = sb("warm_out", [P, 1], F32)
@@ -54,6 +54,8 @@ def tile_attend_spanread_kernel(tc, query, keys_words, keys_scales, kind, size, 
 
         nc.sync.dma_start(slot_list[:], offs)
         nc.sync.dma_start(kind_list[:], offs2)
+        kind_pool = sb("kind_pool", [P, U], F32)
+        nc.sync.dma_start(kind_pool[:], kind)
         for quad in range(4):
             nc.sync.dma_start(
                 key_bytes[32 * quad : 32 * quad + 4, :].bitcast(I32),
@@ -73,8 +75,6 @@ def tile_attend_spanread_kernel(tc, query, keys_words, keys_scales, kind, size, 
             nc.sync.dma_start(staged[h][:], vals[rows, h * (T // 2) : (h + 1) * (T // 2)])
 
         load_half(0)
-        kind_pool = sb("kind_pool", [P, U], F32)
-        nc.sync.dma_start(kind_pool[:], kind)
         size_col = sb("size_col", [P, PASSES, PACK], F32)
         nc.sync.dma_start(size_col[:], size.rearrange("o (g p t) -> p (o g) t", g=PASSES, t=PACK))
 

from contextlib import ExitStack

import concourse.mybir as mybir
from concourse.masks import make_identity

D, T, I, Q, E, G, U = 512, 2048, 1024, 128, 512, 128, 512
FLOPS = 2 * Q * I * D + 2 * Q * I * E

F32 = mybir.dt.float32
BF16 = mybir.dt.bfloat16
I32 = mybir.dt.int32
U32 = mybir.dt.uint32
U16 = mybir.dt.uint16
U8 = mybir.dt.uint8
FP8X4 = mybir.dt.float8_e4m3fn_x4
ALU = mybir.AluOpType
ACT = mybir.ActivationFunctionType
AX = mybir.AxisListType

P = 128
PACK = 4
PASS = P * PACK
PASSES = I // PASS
SPAN = I // G
BLOCKS = E // P
LIST_COLS = PASS // 16
HALF = E // 2
SCALAR_BLOCK, FIRST, SECOND, LAST = 2, 0, 1, 3


def tile_attend_spanread_kernel(tc, query, keys_words, keys_scales, kind, size, vals, offs, offs2, out):
    nc = tc.nc
    with ExitStack() as ctx:
        keep = ctx.enter_context(tc.tile_pool(name="keep", bufs=1))
        psum = ctx.enter_context(tc.psum_pool(name="psum", bufs=1))

        def sb(name, shape, dtype, tag=None):
            return keep.tile(shape, dtype, name=name, tag=tag or name, align_bytes=64)

        slot_list = keep.tile([P, I // 16], U16, name="slot_list")
        kind_list = keep.tile([P, G // 16], U16, name="kind_list")

        def slots(g):
            return slot_list[:, g * LIST_COLS : (g + 1) * LIST_COLS]

        key_bytes = sb("key_bytes", [P, T], U8)
        nc.vector.memset(key_bytes[:].bitcast(I32), 0)
        warm = sb("warm", [P, 1], F32)
        nc.gpsimd.memset(warm[:], 0.0)
        warm_out = sb("warm_out", [P, 1], F32)
        nc.scalar.activation(warm_out[:], warm[:], ACT.Exp)
        identity = sb("identity", [P, P], F32)
        make_identity(nc, identity[:])

        nc.sync.dma_start(slot_list[:], offs)
        nc.sync.dma_start(kind_list[:], offs2)
        kind_pool = sb("kind_pool", [P, U], F32)
        nc.sync.dma_start(kind_pool[:], kind)
        for quad in range(4):
            nc.sync.dma_start(
                key_bytes[32 * quad : 32 * quad + 4, :].bitcast(I32),
                keys_scales[0, 4 * quad : 4 * quad + 4, :].bitcast(I32),
            )
        key_words = sb("key_words", [P, T], I32)
        nc.sync.dma_start(key_words[:], keys_words[0].rearrange("p n t -> p (n t)").bitcast(I32))
        query_raw = sb("query_raw", [P, PACK, Q], F32)
        nc.sync.dma_start(query_raw[:], query.rearrange("(p j) q -> p j q", j=PACK))

        windows = {}
        staged = {}

        def load_half(h):
            staged[h] = sb("stage%d" % h, [P, T // 2], F32)
            rows = slice(SCALAR_BLOCK * P, (SCALAR_BLOCK + 1) * P)
            nc.sync.dma_start(staged[h][:], vals[rows, h * (T // 2) : (h + 1) * (T // 2)])

        load_half(0)
        size_col = sb("size_col", [P, PASSES, PACK], F32)
        nc.sync.dma_start(size_col[:], size.rearrange("o (g p t) -> p (o g) t", g=PASSES, t=PACK))

        def load_block(b):
            windows[b] = sb("window%d" % b, [P, T], F32)
            nc.sync.dma_start(windows[b][:], vals[b * P : (b + 1) * P, :])

        load_half(1)
        load_block(FIRST)
        load_block(SECOND)
        load_block(LAST)
        windows[SCALAR_BLOCK] = sb("window_cast", [P, T], BF16)

        def cast_half(h):
            nc.scalar.activation(windows[SCALAR_BLOCK][:, h * (T // 2) : (h + 1) * (T // 2)], staged[h][:], ACT.Copy)

        picked = {}

        def gather_values(b):
            if b == SCALAR_BLOCK:
                picked[b] = sb("picked%d" % b, [P, I], BF16)
                nc.scalar.activation(picked[b][:], windows[b][:].indirect(slot_list[:]), ACT.Copy)
            else:
                picked[b] = sb("picked%d" % b, [P, I], BF16)
                nc.vector.tensor_copy(picked[b][:], windows[b][:].indirect(slot_list[:]))


        def turn_values(b, bank_tag):
            bank = psum.tile([P, PASSES, 2, P], F32, name="v_bank%d" % b, tag=bank_tag)
            words = picked[b][:].bitcast(F32)
            for g in range(PASSES):
                for u in range(2):
                    nc.tensor.transpose(bank[:, g, u, :], words[:, 2 * P * g + u : 2 * P * (g + 1) : 2], identity[:])
            nc.scalar.copy(grouped[:, :, b * P : (b + 1) * P, :], bank[:].rearrange("p g u e -> p g e u"))

        def quantise_values(g, first, width):
            codes = sb("v_codes%d_%d" % (g, first), [P, width], U32)
            scales = sb("v_scales%d_%d" % (g, first), [P, width], U8)
            nc.vector.quantize_mx(
                out=codes[:].bitcast(FP8X4),
                scales=scales[:],
                in_=late[:, 2 * (g * E + first) : 2 * (g * E + first + width)].bitcast(BF16),
            )
            return codes, scales

        query_grouped = sb("query_grouped", [P, Q, PACK], BF16)
        nc.scalar.activation(query_grouped[:], query_raw[:].rearrange("p j q -> p q j"), ACT.Copy)

        picked_bytes = sb("picked_bytes", [P, I], U8)
        nc.vector.tensor_copy(picked_bytes[:], key_bytes[:].indirect(slot_list[:]))
        picked_words = [sb("picked_words0", [P, PASS], U32)]
        q_codes = sb("q_codes", [P, Q], U32)
        q_scales = sb("q_scales", [P, Q], U8)
        nc.vector.tensor_copy(picked_words[0][:], key_words[:].bitcast(U32).indirect(slots(0)))
        nc.vector.quantize_mx(
            out=q_codes[:].bitcast(FP8X4), scales=q_scales[:], in_=query_grouped[:].rearrange("p q j -> p (q j)")
        )
        picked_words.append(sb("picked_words1", [P, PASS], U32, "query_grouped"))
        nc.vector.tensor_copy(picked_words[1][:], key_words[:].bitcast(U32).indirect(slots(1)))
        scores = [psum.tile([P, PASS], F32, name="scores%d" % g, tag="bank%d" % g) for g in range(PASSES)]
        for g in range(PASSES):
            nc.tensor.matmul_mx(
                out=scores[g][:],
                lhsT=q_codes[:].bitcast(FP8X4),
                lhsT_scale=q_scales[:],
                rhs=picked_words[g][:].bitcast(FP8X4),
                rhs_scale=picked_bytes[:, g * PASS : (g + 1) * PASS],
                start=True,
                stop=True,
            )

        cast_half(0)
        picked_kind = sb("picked_kind", [P, G], F32)
        nc.vector.tensor_copy(picked_kind[:], kind_pool[:].indirect(kind_list[:]))

        span_sum = sb("span_sum", [P, G], F32)
        for g in range(PASSES):
            nc.vector.tensor_reduce(
                span_sum[:, g * (G // PASSES) : (g + 1) * (G // PASSES)],
                scores[g][:].rearrange("p (s j) -> p s j", j=SPAN),
                AX.X,
                ALU.add,
            )
        logits = sb("logits", [P, G], F32)
        nc.vector.scalar_tensor_tensor(logits[:], span_sum[:], 1.0 / SPAN, picked_kind[:], ALU.mult, ALU.add)
        minus_max = sb("minus_max", [P, 1], F32)
        nc.vector.tensor_reduce(minus_max[:], logits[:], AX.X, ALU.max, negate=True)

        cast_half(1)
        gather_values(SCALAR_BLOCK)
        widths = (PASSES * 2 * E, I, I, 2 * G, G)
        late = sb("late", [P, sum(widths)], F32, "window_cast")
        parts = [late[:, sum(widths[:k]) : sum(widths[: k + 1])] for k in range(len(widths))]
        grouped = parts[0].rearrange("p (g e u) -> p g e u", g=PASSES, u=2)
        gates = parts[1].rearrange("p (g t s) -> p g t s", g=PASSES, t=PACK)
        sized = parts[2].rearrange("p (g t q) -> p g t q", g=PASSES, t=PACK)
        twice = parts[3]
        span_exp = parts[4]

        row_sum = sb("row_sum", [P, 1], F32)
        nc.scalar.activation(span_exp, logits[:], ACT.Exp, bias=minus_max[:], accum_out=row_sum[:])
        gates_turned = [psum.tile([P, PACK, Q], F32, name="gates_turned%d" % g, tag="bank%d" % (2 + g)) for g in range(PASSES)]
        for g in range(PASSES):
            nc.scalar.activation(gates[:, g], scores[g][:].rearrange("p (s t) -> p t s", t=PACK), ACT.Sigmoid)
            for t in range(PACK):
                nc.tensor.transpose(gates_turned[g][:, t, :], gates[:, g, t, :], identity[:])

        gather_values(FIRST)
        inv_sum = sb("inv_sum", [P, 1], F32, "window%d" % FIRST)
        nc.vector.reciprocal(inv_sum[:], row_sum[:])
        nc.scalar.activation(
            twice.rearrange("p (s k) -> p s k", k=2),
            span_exp.unsqueeze(2).to_broadcast([P, G, 2]),
            ACT.Copy,
            scale=inv_sum[:],
        )
        weight_turned = psum.tile([P, PASSES, Q], F32, name="weight_turned", tag="bank4")
        for g in range(PASSES):
            nc.tensor.transpose(weight_turned[:, g, :], twice[:, g * P : (g + 1) * P], identity[:])
        turn_values(FIRST, "bank5")
        for g in range(PASSES):
            for t in range(PACK):
                nc.scalar.activation(
                    sized[:, g, t, :], gates_turned[g][:, t, :], ACT.Copy, scale=size_col[:, g, t : t + 1]
                )
        turn_values(SCALAR_BLOCK, "bank7")
        gather_values(SECOND)
        turn_values(SECOND, "bank6")
        for g in range(PASSES):
            part = sb("picked_last%d" % g, [P, PASS], BF16)
            nc.vector.tensor_copy(part[:], windows[LAST][:].indirect(slots(g)))
            bank = psum.tile([P, 2, P], F32, name="last_bank%d" % g, tag="bank%d" % g)
            words = part[:].bitcast(F32)
            for u in range(2):
                nc.tensor.transpose(bank[:, u, :], words[:, u : 2 * P : 2], identity[:])
            nc.scalar.copy(grouped[:, g, LAST * P : (LAST + 1) * P, :], bank[:].rearrange("p u e -> p e u"))

        w_grouped = sb("w_grouped", [P, PASSES, Q, PACK], BF16, "window%d" % LAST)
        nc.vector.tensor_tensor(
            w_grouped[:],
            sized.rearrange("p g t q -> p g q t"),
            weight_turned[:].unsqueeze(3).to_broadcast([P, PASSES, Q, PACK]),
            ALU.mult,
        )
        first_codes, first_scales = quantise_values(0, 0, E)
        w_codes = sb("w_codes", [P, PASSES * Q], U32)
        w_scales = sb("w_scales", [P, PASSES * Q], U8)
        nc.vector.quantize_mx(
            out=w_codes[:].bitcast(FP8X4), scales=w_scales[:], in_=w_grouped[:].rearrange("p g q t -> p (g q t)")
        )
        groups = ((0, HALF), (HALF, P), (HALF + P, P))
        sums = [psum.tile([P, width], F32, name="sums%d" % k, tag="bank%d" % (2 + k)) for k, (first, width) in enumerate(groups)]

        def multiply(g, k, codes, scales):
            nc.tensor.matmul_mx(
                out=sums[k][:],
                lhsT=w_codes[:, g * Q : (g + 1) * Q].bitcast(FP8X4),
                lhsT_scale=w_scales[:, g * Q : (g + 1) * Q],
                rhs=codes.bitcast(FP8X4),
                rhs_scale=scales,
                start=(g == 0),
                stop=(g == PASSES - 1),
            )

        for k, (first, width) in enumerate(groups):
            multiply(0, k, first_codes[:, first : first + width], first_scales[:, first : first + width])
        for k, (first, width) in enumerate(groups):
            codes, scales = quantise_values(1, first, width)
            multiply(1, k, codes[:], scales[:])
        result = [sb("result%d" % h, [P, HALF], F32) for h in range(2)]
        nc.scalar.copy(result[0][:], sums[0][:])
        nc.sync.dma_start(out[:, 0:HALF], result[0][:])
        nc.scalar.copy(result[1][:, 0:P], sums[1][:])
        nc.vector.tensor_copy(result[1][:, P:HALF], sums[2][:])
        nc.sync.dma_start(out[:, HALF:E], result[1][:])
